import numpy as np
import ml_dtypes


def mxq(x, axis, fmt="e4m3"):
    dtype, down = {"e4m3": (ml_dtypes.float8_e4m3fn, 7), "e5m2": (ml_dtypes.float8_e5m2, 14)}[fmt]
    v = np.moveaxis(np.asarray(x, np.float32).astype(ml_dtypes.bfloat16).astype(np.float64), axis, -1)
    blocks = v.reshape(v.shape[:-1] + (-1, 32))
    amax = np.abs(blocks).max(-1, keepdims=True)
    byte = np.maximum(np.where(amax > 0, np.frexp(amax)[1] - 1 + 127, 0) - down, 1)
    scale = np.exp2(byte - 127.0)
    codes = (blocks / scale).astype(np.float32).astype(dtype).astype(np.float64)
    return np.moveaxis((codes * scale).reshape(v.shape), -1, axis)


WIDE = False


def mx_kscale(k):
    if not WIDE:
        return np.ones(k)
    levels = np.array([10, -10, 5, -5, 0])
    if k % 512:
        return np.exp2(np.random.permutation(np.resize(levels, k // 32))).repeat(32)
    a = np.empty((k // 512, 16))
    for p in range(k // 512):
        a[p, :8] = np.random.permutation(np.resize(levels, 8))
        for g in range(8):
            far = levels[np.abs(levels - a[p, g]) >= 10]
            a[p, g + 8] = far[np.random.randint(len(far))]
    return np.exp2(a.ravel()).repeat(32)


BF16 = ml_dtypes.bfloat16


def bf(x):
    return np.asarray(x, np.float32).astype(BF16)


def f64(x):
    return np.asarray(x).astype(np.float64)


E2M1 = np.array([0.0, 0.5, 1.0, 1.5, 2.0, 3.0, 4.0, 6.0, -0.0, -0.5, -1.0, -1.5, -2.0, -3.0, -4.0, -6.0])


def pack_weight(w, fmt):
    k, n = w.shape
    w = f64(bf(w)).reshape(k // 32, 32, n)
    amax = np.abs(w).max(1)
    if fmt == "e4m3":
        byte = np.frexp(amax)[1] - 1 + 127 - 7
    else:
        mant, ex = np.frexp(amax / 6.0)
        byte = np.where(mant > 0.5, ex, ex - 1) + 127
    byte = np.clip(np.where(amax > 0, byte, 1), 1, 254)
    scaled = (w * np.exp2(127.0 - byte)[:, None, :]).reshape(k, n).astype(np.float32)
    by_word = np.ascontiguousarray(scaled.reshape(k // 512, 128, 4, n).transpose(0, 1, 3, 2))
    if fmt == "e4m3":
        words = by_word.astype(ml_dtypes.float8_e4m3fn).view(np.uint8)
    else:
        c = by_word.astype(ml_dtypes.float4_e2m1fn).view(np.uint8) & 0xF
        words = c[..., 0::2] | (c[..., 1::2] << 4)
    return np.ascontiguousarray(words), np.ascontiguousarray(byte.astype(np.uint8).reshape(k // 512, 16, n))


def unpack_weight(words, scales, fmt):
    g, p, n, _ = words.shape
    if fmt == "e4m3":
        vals = np.ascontiguousarray(words).view(ml_dtypes.float8_e4m3fn).astype(np.float64)
    else:
        nib = np.empty((g, p, n, 4), np.uint8)
        nib[..., 0::2] = words & 0xF
        nib[..., 1::2] = words >> 4
        vals = E2M1[nib]
    vals = vals * np.repeat(np.exp2(scales.astype(np.float64) - 127.0), 8, axis=1)[..., None]
    return vals.transpose(0, 1, 3, 2).reshape(g * 512, n)
def pack4(w):
    words, scales = pack_weight(w, "e2m1")
    return words.reshape(words.shape[0], 128, -1), scales


def unpack4(words, scales):
    return unpack_weight(words.reshape(words.shape[0], 128, -1, 2), scales, "e2m1")


def planes(Y):
    n, m = Y.shape
    b = f64(bf(Y)).reshape(n // 32, 32, m)
    amax = np.abs(b).max(1)
    byte = np.clip(np.where(amax > 0, np.frexp(amax)[1] - 1 + 127 - 7, 1), 1, 254)
    codes = (b * np.exp2(127.0 - byte)[:, None, :]).reshape(n, m).astype(np.float32).astype(ml_dtypes.float8_e4m3fn).view(np.uint8)
    words = codes.reshape(n // 512, 128, 4, m).transpose(0, 1, 3, 2)
    return np.ascontiguousarray(words), np.ascontiguousarray(byte.astype(np.uint8).reshape(n // 512, 16, m))


B, S, M, D = 2, 512, 1024, 1024


def softmax(x):
    e = np.exp(x - x.max(-1, keepdims=True))
    return e / e.sum(-1, keepdims=True)


def sigmoid(x):
    return 1.0 / (1.0 + np.exp(-x))


def setup_inputs():
    s, t = mx_kscale(D), mx_kscale(M)
    u = bf(np.random.standard_normal((B, S, D)))
    m = bf((1.0 + 0.1 * np.random.standard_normal(D)) * s)
    keys = bf(np.random.standard_normal((B, M, D)) * 2.0 / np.sqrt(D) / s)
    vals = bf(np.random.standard_normal((B, M, D)) * np.sqrt(M) / 16.0 / t[:, None])
    g = bf(np.random.standard_normal(M) * t)
    wt_words, wt_scales = pack4(np.random.standard_normal((D, D)) / np.sqrt(D) / s[:, None])
    bt = bf(np.random.standard_normal(D) * 0.5)
    return {
        "u": u,
        "m": m,
        "keys": keys,
        "vals": vals,
        "g": g,
        "wt_words": wt_words,
        "wt_scales": wt_scales,
        "bt": bt,
    }


def read_memory(vq, keys, vals, g):
    scores = vq @ mxq(f64(keys), 2, "e4m3").transpose(0, 2, 1)
    p = softmax(scores)
    pg = p * f64(g)[None, None, :]
    return mxq(pg, 2, "e4m3") @ mxq(f64(vals), 1, "e4m3")


def core(u, m, keys, vals, g, wt_words, wt_scales, bt):
    v = f64(u) * f64(m)[None, None, :]
    vq = mxq(v, 2, "e4m3")
    o = read_memory(vq, keys, vals, g)
    t = sigmoid((vq @ unpack4(wt_words, wt_scales)) + f64(bt))
    return t * o + (1.0 - t) * f64(u)


def reference(u, m, keys, vals, g, wt_words, wt_scales, bt):
    R_out = core(u, m, keys, vals, g, wt_words, wt_scales, bt)
    words, scales = planes(np.moveaxis(R_out, 1, 0).reshape(512, -1))
    return R_out, words, scales

from contextlib import ExitStack

import concourse.mybir as mybir
from concourse.masks import make_identity

B, S, M, D = 2, 512, 1024, 1024
P = 128
HALF = 512

F32 = mybir.dt.float32
BF16 = mybir.dt.bfloat16
I32 = mybir.dt.int32
U32 = mybir.dt.uint32
U8 = mybir.dt.uint8
FP8 = mybir.dt.float8_e4m3fn_x4
FP4 = mybir.dt.float4_e2m1fn_x4
ALU = mybir.AluOpType
ACT = mybir.ActivationFunctionType
AX = mybir.AxisListType

FLOPS = 3 * 2 * B * S * M * D


def tile_gatedmemn2nhopsignedslots_x2_kernel(tc, u, m, keys, vals, g, wt_words, wt_scales, bt, out_0, out_1, out_2):
    nc = tc.nc
    with ExitStack() as ctx:
        const = ctx.enter_context(tc.tile_pool(name="const", bufs=1))
        sb = ctx.enter_context(tc.tile_pool(name="sb", bufs=2))
        ps = ctx.enter_context(tc.psum_pool(name="ps", bufs=2))

        row_m = sb.tile([P, D], BF16, name="row_m", tag="pg", bufs=2, align_bytes=64)
        row_g = sb.tile([P, D], BF16, name="row_g", tag="pg", bufs=2, align_bytes=64)
        sel = const.tile([P, P], BF16, name="sel", align_bytes=64)
        bt_rows = const.tile([P, P], BF16, name="bt_rows", align_bytes=64)
        warm = const.tile([P, 1], F32, name="warm")
        nc.vector.memset(warm[:], 0.0)
        nc.vector.memset(row_m[:], 0.0)
        nc.vector.memset(row_g[:], 0.0)
        nc.vector.memset(sel[:], 0.0)
        nc.vector.memset(sel[0:1, :], 1.0)
        nc.vector.memset(bt_rows[:], 0.0)
        w_sc = const.tile([P, 2, D], U8, name="w_sc", align_bytes=64)
        nc.vector.memset(w_sc[:].rearrange("p a b -> p (a b)").bitcast(I32), 0)
        nc.sync.dma_start(out=row_m[0:1, :], in_=m.rearrange("(o d) -> o d", o=1))

        u_sb = []
        k_raw = {}
        v_raw = {}

        def load_u(b):
            t_u = const.tile([P, 4, D], BF16, name="u_sb%d" % b, align_bytes=64)
            src = u[b].rearrange("(p t) d -> p t d", t=4)
            n = 1 if b == 0 else 2
            for x in range(0, 4, n):
                nc.sync.dma_start(out=t_u[:, x : x + n, :], in_=src[:, x : x + n, :])
            u_sb.append(t_u)

        def load_k(b, h):
            t_k = sb.tile([P, 4, D], BF16, name="k_raw%d%d" % (b, h), tag="k_raw", bufs=3, align_bytes=64)
            src = keys[b, HALF * h : HALF * (h + 1), :].rearrange("(p t) d -> p t d", t=4)
            n = 1 if b == 0 and h == 0 else 2
            for x in range(0, 4, n):
                nc.sync.dma_start(out=t_k[:, x : x + n, :], in_=src[:, x : x + n, :])
            k_raw[b, h] = t_k

        def load_v(b, a):
            t_v = sb.tile([P, 4, D], BF16, name="v_raw%d%d" % (b, a), tag="v_raw", bufs=2, align_bytes=64)
            src = vals[b, HALF * a : HALF * (a + 1), :].rearrange("(p t) d -> p t d", t=4)
            nc.sync.dma_start(out=t_v[:], in_=src)
            v_raw[b, a] = t_v

        load_k(0, 0)
        load_u(0)
        load_k(0, 1)
        nc.sync.dma_start(out=row_g[0:1, :], in_=g.rearrange("(o d) -> o d", o=1))
        nc.sync.dma_start(out=bt_rows[0:8, :], in_=bt.rearrange("(c p) -> c p", c=8))
        w_sb = const.tile([P, 2, 2 * D], U8, name="w_sb", align_bytes=64)
        nc.sync.dma_start(
            out=w_sb[:].rearrange("p a b -> p (a b)").bitcast(I32).rearrange("p (a b) -> p a b", a=2),
            in_=wt_words.bitcast(I32).rearrange("a p b -> p a b"),
        )
        w_sc_i = w_sc[:].rearrange("p a b -> p (a b)").bitcast(I32).rearrange("p (a b) -> p a b", a=2)
        wt_sc_i = wt_scales.bitcast(I32)
        for q in range(4):
            nc.sync.dma_start(out=w_sc_i[32 * q : 32 * q + 4], in_=wt_sc_i[:, 4 * q : 4 * q + 4, :].rearrange("a r n -> r a n"))
        load_u(1)
        load_k(1, 0)
        load_k(1, 1)
        load_v(0, 0)
        load_v(0, 1)
        load_v(1, 0)
        load_v(1, 1)

        warm2 = const.tile([P, 1], F32, name="warm2")
        nc.scalar.activation(out=warm2[:], in_=warm[:], func=ACT.Exp)
        id_f = const.tile([P, P], F32, name="id_f", align_bytes=64)
        make_identity(nc, id_f[:])
        id_b = const.tile([P, P], BF16, name="id_b", align_bytes=64)
        make_identity(nc, id_b[:])

        m_bc = const.tile([P, D], BF16, name="m_bc", align_bytes=64)
        g_bc = const.tile([P, M], BF16, name="g_bc", align_bytes=64)
        bth = const.tile([P, 8], F32, name="bth")

        def consts_m():
            for h in range(2):
                cols = slice(HALF * h, HALF * (h + 1))
                bank = ps.tile([P, HALF], F32, name="bank_m%d" % h, tag="tp", bufs=2)
                nc.tensor.matmul(out=bank[:], lhsT=sel[:], rhs=row_m[:, cols], start=True, stop=True)
                if h == 0:
                    nc.scalar.copy(out=m_bc[:, cols], in_=bank[:])
                else:
                    nc.vector.tensor_copy(out=m_bc[:, cols], in_=bank[:])

        def consts_g():
            for h in range(2):
                cols = slice(HALF * h, HALF * (h + 1))
                bank = ps.tile([P, HALF], F32, name="bank_g%d" % h, tag="mm", bufs=2)
                nc.tensor.matmul(out=bank[:], lhsT=sel[:], rhs=row_g[:, cols], start=True, stop=True)
                nc.scalar.copy(
                    out=g_bc[:, cols].rearrange("p (a q e) -> p a q e", a=2, e=2),
                    in_=bank[:].rearrange("p (q a e) -> p a q e", a=2, e=2),
                )
            bank_bt = ps.tile([P, P], BF16, name="bank_bt", tag="mm", bufs=2)
            nc.tensor.transpose(bank_bt[:], bt_rows[:], id_b[:])
            nc.vector.tensor_scalar(out=bth[:], in0=bank_bt[:, 0:8], scalar1=0.5, scalar2=None, op0=ALU.mult)

        v_g = {}
        v_c = {}
        v_s = {}
        k_g = {}
        k_c = {}
        k_s = {}
        x_c = {}
        x_s = {}
        p_c = {}
        p_s = {}
        thT = {}

        def words_out(eng, dst, bank):
            src = bank[:].rearrange("p a c r -> p a r c")
            if eng == "s":
                nc.scalar.copy(out=dst, in_=src)
            else:
                nc.vector.tensor_copy(out=dst, in_=src)

        def tp_words(bank, words):
            for a in range(2):
                for c in range(2):
                    nc.tensor.transpose(bank[:, a, c, :], words[:, 256 * a + c : 256 * (a + 1) : 2], id_f[:])

        uh = {}
        vbs = {}

        def half_u(b, h):
            uh[b, h] = sb.tile([P, 4, HALF], BF16, name="uh", tag="uh", bufs=3, align_bytes=64)
            nc.vector.tensor_scalar(out=uh[b, h][:], in0=u_sb[b][:, :, HALF * h : HALF * (h + 1)], scalar1=0.5, scalar2=None, op0=ALU.mult)

        def stage_u(b, t):
            if t == 0:
                v_g[b] = sb.tile([P, 2 * S * 4], BF16, name="v_g%d" % b, tag="k_g", bufs=2, align_bytes=64)
                v_c[b] = const.tile([P, 2, S], U32, name="v_c%d" % b, align_bytes=64)
                v_s[b] = const.tile([P, 2, S], U8, name="v_s%d" % b, align_bytes=64)
            vb = sb.tile([P, D], BF16, name="vb", tag="vb", bufs=2, align_bytes=64)
            nc.vector.tensor_tensor(out=vb[:], in0=u_sb[b][:, t, :], in1=m_bc[:], op=ALU.mult)
            vbs[b, t] = vb

        def stage_u2(b, t):
            vb = vbs[b, t]
            bank = ps.tile([P, 2, 2, P], F32, name="bank_u", tag="tp", bufs=2)
            tp_words(bank, vb[:].bitcast(F32))
            dst = v_g[b][:].bitcast(F32).rearrange("p (a n c) -> p a n c", a=2, c=2)[:, :, P * t : P * (t + 1), :]
            words_out("s", dst, bank)

        def quant_u(b):
            for a in range(2):
                nc.vector.quantize_mx(out=v_c[b][:, a, :].bitcast(FP8), scales=v_s[b][:, a, :], in_=v_g[b][:, 4 * S * a : 4 * S * (a + 1)])

        def stage_k(b, h, t, eng):
            if t == 0:
                k_g[b, h] = sb.tile([P, 2 * HALF * 4], BF16, name="k_g", tag="k_g", bufs=2, align_bytes=64)
                k_c[b, h] = sb.tile([P, 2, HALF], U32, name="k_c", tag="k_c", bufs=3, align_bytes=64)
                k_s[b, h] = sb.tile([P, 2, HALF], U8, name="k_s", tag="k_s", bufs=3, align_bytes=64)
            bank = ps.tile([P, 2, 2, P], F32, name="bank_k", tag="sc" if b == 0 else "tp", bufs=4 if b == 0 else 2)
            tp_words(bank, k_raw[b, h][:, t, :].bitcast(F32))
            dst = k_g[b, h][:].bitcast(F32).rearrange("p (a n c) -> p a n c", a=2, c=2)[:, :, P * t : P * (t + 1), :]
            words_out(eng, dst, bank)

        def quant_k(b, h):
            for a in range(2):
                nc.vector.quantize_mx(out=k_c[b, h][:, a, :].bitcast(FP8), scales=k_s[b, h][:, a, :], in_=k_g[b, h][:, 4 * HALF * a : 4 * HALF * (a + 1)])

        x_g = {}

        def stage_x(b, a, x, eng):
            if x == 0:
                x_c[b, a] = sb.tile([P, D], U32, name="x_c", tag="x_c", bufs=3, align_bytes=64)
                x_s[b, a] = sb.tile([P, D], U8, name="x_s", tag="x_s", bufs=3, align_bytes=64)
            t_g = sb.tile([P, HALF, 4], BF16, name="x_g", tag="x_g", bufs=2, align_bytes=64)
            src = v_raw[b, a][:, :, HALF * x : HALF * (x + 1)].rearrange("p t c -> p c t")
            if eng == "s":
                nc.scalar.copy(out=t_g[:], in_=src)
            elif eng == "g":
                nc.gpsimd.tensor_scalar(out=t_g[:], in0=src, scalar1=1.0, scalar2=0.0, op0=ALU.mult, op1=ALU.add)
            else:
                nc.vector.tensor_copy(out=t_g[:], in_=src)
            x_g[b, a, x] = t_g

        def quant_x(b, a, x):
            cols = slice(HALF * x, HALF * (x + 1))
            nc.vector.quantize_mx(out=x_c[b, a][:, cols].bitcast(FP8), scales=x_s[b, a][:, cols], in_=x_g[b, a, x][:].rearrange("p c t -> p (c t)"))

        def stage_gate(b, c):
            h = c // 4
            if c % 4 == 0:
                thT[b, h] = sb.tile([P, 4, S], F32, name="thT", tag="thT", bufs=3, align_bytes=64)
            bank = ps.tile([P, S], F32, name="bank_w", tag="mm", bufs=2)
            for a in range(2):
                nc.tensor.matmul_mx(
                    out=bank[:],
                    lhsT=w_sb[:, a, 2 * P * c : 2 * P * (c + 1)].bitcast(FP4),
                    lhsT_scale=w_sc[:, a, P * c : P * (c + 1)],
                    rhs=v_c[b][:, a, :].bitcast(FP8),
                    rhs_scale=v_s[b][:, a, :],
                    start=(a == 0),
                    stop=(a == 1),
                )
            nc.scalar.activation(out=thT[b, h][:, c % 4, :], in_=bank[:], func=ACT.Tanh, bias=bth[:, c : c + 1], scale=0.5)

        st = {}

        def soft1a(b, t):
            mx = sb.tile([P, 2], F32, name="mx", tag="mx", bufs=3)
            nm = sb.tile([P, 1], F32, name="nm", tag="nm", bufs=3)
            sm = sb.tile([P, 2], F32, name="sm", tag="sm", bufs=3)
            e = sb.tile([P, M], F32, name="e", tag="e", bufs=2, align_bytes=64)
            banks = []
            for h in range(2):
                bank = ps.tile([P, HALF], F32, name="bank_s", tag="sc", bufs=4)
                for a in range(2):
                    nc.tensor.matmul_mx(
                        out=bank[:],
                        lhsT=v_c[b][:, a, P * t : P * (t + 1)].bitcast(FP8),
                        lhsT_scale=v_s[b][:, a, P * t : P * (t + 1)],
                        rhs=k_c[b, h][:, a, :].bitcast(FP8),
                        rhs_scale=k_s[b, h][:, a, :],
                        start=(a == 0),
                        stop=(a == 1),
                    )
                banks.append(bank)
            st[b, t] = (mx, nm, sm, e, banks)

        def soft1b(b, t, h):
            mx, nm, sm, e, banks = st[b, t]
            nc.vector.tensor_reduce(out=mx[:, h : h + 1], in_=banks[h][:], axis=AX.X, op=ALU.max)

        def soft1n(b, t):
            mx, nm, sm, e, banks = st[b, t]
            nc.vector.tensor_scalar(out=nm[:], in0=mx[:, 0:1], scalar1=mx[:, 1:2], scalar2=-1.0, op0=ALU.max, op1=ALU.mult)

        def soft1c(b, t):
            mx, nm, sm, e, banks = st[b, t]
            for h in range(2):
                nc.scalar.activation(
                    out=e[:, HALF * h : HALF * (h + 1)].rearrange("p (a q e) -> p a q e", a=2, e=2),
                    in_=banks[h][:].rearrange("p (a e q) -> p a q e", a=2, e=2),
                    func=ACT.Exp,
                    bias=nm[:],
                    scale=1.0,
                    accum_out=sm[:, h : h + 1],
                )

        pgs = {}

        rss = {}

        def soft2s(b, t):
            mx, nm, sm, e, banks = st[b, t]
            ss = sb.tile([P, 1], F32, name="ss", tag="ss", bufs=3)
            nc.vector.tensor_tensor(out=ss[:], in0=sm[:, 0:1], in1=sm[:, 1:2], op=ALU.add)
            rss[b, t] = ss

        def soft2r(b, t):
            rs = sb.tile([P, 1], F32, name="rs", tag="rs", bufs=3)
            nc.vector.reciprocal(out=rs[:], in_=rss[b, t][:])
            rss[b, t] = rs

        def soft2(b, t):
            mx, nm, sm, e, banks = st[b, t]
            rs = rss[b, t]
            pg = sb.tile([P, M], BF16, name="pg", tag="pg", bufs=2, align_bytes=64)
            nc.vector.scalar_tensor_tensor(
                out=pg[:],
                in0=e[:],
                scalar=rs[:],
                in1=g_bc[:],
                op0=ALU.mult,
                op1=ALU.mult,
            )
            pgs[b, t] = pg

        def soft3(b, t):
            words = pgs[b, t][:].bitcast(F32)
            bank = ps.tile([P, 2, 2, P], F32, name="bank_p", tag="tp", bufs=2)
            for a in range(2):
                for c in range(2):
                    j = 2 * a + c
                    nc.tensor.transpose(bank[:, a, c, :], words[:, P * j : P * (j + 1)], id_f[:])
            p_g = sb.tile([P, 2 * P * 4], BF16, name="p_g", tag="p_g", bufs=2, align_bytes=64)
            words_out("s", p_g[:].bitcast(F32).rearrange("p (a n c) -> p a n c", a=2, c=2), bank)
            p_c[b, t] = sb.tile([P, 2 * P], U32, name="p_c", tag="p_c", bufs=8, align_bytes=64)
            p_s[b, t] = sb.tile([P, 2 * P], U8, name="p_s", tag="p_s", bufs=8, align_bytes=64)
            pgs[b, t] = p_g

        def soft4(b, t):
            nc.vector.quantize_mx(out=p_c[b, t][:].bitcast(FP8), scales=p_s[b, t][:], in_=pgs[b, t][:])

        outs = {}
        fin = {}

        def final(b, h, t):
            if t == 0:
                outs[b, h] = sb.tile([P, 4, HALF], F32, name="o_f", tag="o_f", bufs=2, align_bytes=64)
            cols = slice(HALF * h, HALF * (h + 1))
            bank = ps.tile([P, HALF], F32, name="bank_o", tag="sc", bufs=4)
            for a in range(2):
                nc.tensor.matmul_mx(
                    out=bank[:],
                    lhsT=p_c[b, t][:, P * a : P * (a + 1)].bitcast(FP8),
                    lhsT_scale=p_s[b, t][:, P * a : P * (a + 1)],
                    rhs=x_c[b, a][:, cols].bitcast(FP8),
                    rhs_scale=x_s[b, a][:, cols],
                    start=(a == 0),
                    stop=(a == 1),
                )
            fin[b, h, t] = bank

        def final_t(b, h, t):
            bank = fin[b, h, t]
            th = ps.tile([P, 4, P], F32, name="bank_t", tag="mm", bufs=2)
            for c in range(4):
                nc.tensor.transpose(th[:, c, :], thT[b, h][:, c, P * t : P * (t + 1)], id_f[:])
            fin[b, h, t] = (bank, th)

        def final_pair(x, y):
            final(*x)
            final(*y)
            final_t(*x)
            final_t(*y)

        def final_d(b, h, t):
            bank, th = fin[b, h, t]
            cols = slice(HALF * h, HALF * (h + 1))
            d = sb.tile([P, HALF], F32, name="d", tag="d", bufs=2, align_bytes=64)
            nc.vector.scalar_tensor_tensor(out=d[:], in0=bank[:], scalar=0.5, in1=uh[b, h][:, t, :], op0=ALU.mult, op1=ALU.subtract)
            fin[b, h, t] = (d, th)

        def final_e(b, h, t, eng):
            d, th = fin[b, h, t]
            cols = slice(HALF * h, HALF * (h + 1))
            td = sb.tile([P, HALF], F32, name="td", tag="td", bufs=2, align_bytes=64)
            nc.vector.scalar_tensor_tensor(out=td[:], in0=th[:].rearrange("p c r -> p (c r)"), scalar=1.0, in1=d[:], op0=ALU.add, op1=ALU.mult)
            add = nc.gpsimd.tensor_tensor if eng == "g" else nc.vector.tensor_tensor
            add(out=outs[b, h][:, t, :], in0=td[:], in1=u_sb[b][:, t, cols], op=ALU.add)

        def store(b, h, cut):
            o_f = outs[b, h]
            nc.sync.dma_start(out=out_0[b].rearrange("(p t) d -> p t d", t=4)[:, :, HALF * h : HALF * (h + 1)], in_=o_f[:])
            o_b = sb.tile([P, HALF, 4], BF16, name="o_b", tag="o_b", bufs=2, align_bytes=64)
            src = o_f[:].rearrange("p t c -> p c t")
            if cut > 0:
                nc.vector.tensor_copy(out=o_b[:, 0:cut, :], in_=src[:, 0:cut, :])
            nc.scalar.copy(out=o_b[:, cut:HALF, :], in_=src[:, cut:HALF, :])
            o_c = sb.tile([P, HALF], U32, name="o_c", tag="o_c", bufs=2, align_bytes=64)
            o_s = sb.tile([P, HALF], U8, name="o_s", tag="o_s", bufs=2, align_bytes=64)
            fin[b, h] = (o_b, o_c, o_s)

        def store2(b, h):
            o_b, o_c, o_s = fin[b, h]
            nc.vector.quantize_mx(out=o_c[:].bitcast(FP8), scales=o_s[:], in_=o_b[:].rearrange("p c t -> p (c t)"))
            c0 = D * b + HALF * h
            nc.sync.dma_start(out=out_1[0].rearrange("p c t -> p (c t)").bitcast(I32)[:, c0 : c0 + HALF], in_=o_c[:].bitcast(I32))
            sc_i = o_s[:].bitcast(I32)
            out_2_i = out_2[0].bitcast(I32)
            for q in range(4):
                nc.sync.dma_start(out=out_2_i[4 * q : 4 * q + 4, c0 // 4 : (c0 + HALF) // 4], in_=sc_i[32 * q : 32 * q + 4, :])

        if True:
            stage_k(0, 0, 0, "s")
            stage_k(0, 0, 1, "s")
            consts_m()
            stage_k(0, 0, 2, "s")
            stage_k(0, 0, 3, "s")
            for t in range(4):
                stage_u(0, t)
                stage_u2(0, t)
            quant_k(0, 0)
            for t in range(4):
                stage_k(0, 1, t, "ssss"[t])
            quant_u(0)
            quant_k(0, 1)
            consts_g()
            seq = [(0, 0), (0, 1), (0, 2), (0, 3), (1, 0), (1, 1), (1, 2), (1, 3)]
            soft1a(*seq[0])
            soft1b(*seq[0], 0)
            soft1b(*seq[0], 1)
            stage_u(1, 0)
            stage_u(1, 1)
            soft1n(*seq[0])
            soft1c(*seq[0])
            soft1a(*seq[1])
            u_at = [2, 2, 0, 0, 0, 0, 0, 0]
            k_at = [4, 4, 0, 0, 0, 0, 0, 0]
            g_at = [0, 0, 2, 2, 2, 2, 2, 2]
            x_at = ["", "", "v", "v", "s", "v", "s", ""]
            nu, nk, ng, nx = 0, 0, 0, 0
            pend, pend2 = [], []
            for i in range(8):
                nxt = i + 1 < 8
                if nxt:
                    soft1b(*seq[i + 1], 0)
                soft2s(*seq[i])
                if nxt:
                    soft1b(*seq[i + 1], 1)
                soft2r(*seq[i])
                if i < 2:
                    stage_u(1, i + 2)
                elif i == 2:
                    half_u(0, 0)
                elif i == 3:
                    half_u(0, 1)
                elif i == 4:
                    half_u(1, 0)
                pend, now = [], pend
                xs = []
                for eng in x_at[i]:
                    xx = divmod(nx, 4)[0], divmod(nx, 4)[1] // 2, nx % 2
                    nx += 1
                    xs.append(xx)
                    if eng in "vg":
                        stage_x(*xx, eng)
                for f in now:
                    f()
                if nxt:
                    soft1n(*seq[i + 1])
                    soft1c(*seq[i + 1])
                soft2(*seq[i])
                if i + 2 < 8:
                    soft1a(*seq[i + 2])
                for q in range(g_at[i]):
                    stage_gate(ng // 8, ng % 8)
                    ng += 1
                soft3(*seq[i])
                for q in range(u_at[i]):
                    stage_u2(1, nu)
                    nu += 1
                    if nu == 4:
                        pend.append(lambda: quant_u(1))
                for q in range(k_at[i]):
                    stage_k(1, nk // 4, nk % 4, "s")
                    nk += 1
                    if nk % 4 == 0:
                        hh = nk // 4 - 1
                        pend.append(lambda hh=hh: quant_k(1, hh))
                for eng, xx in zip(x_at[i], xs):
                    if eng == "s":
                        stage_x(*xx, "s")
                    pend.append(lambda xx=xx: quant_x(*xx))
                if i > 0:
                    soft4(*seq[i - 1])
            items = [(b, h, t) for b in range(2) for h in range(2) for t in range(4)]
            final_pair(items[0], items[1])
            for f in pend:
                f()
            final_d(*items[0])
            soft4(1, 3)
            pend = []
            nsx = 0
            for i in range(16):
                b, h, t = items[i]
                if i % 2 == 0 and i + 2 < 16:
                    final_pair(items[i + 2], items[i + 3])
                if i + 1 < 16:
                    if i == 3:
                        half_u(1, 1)
                    final_d(*items[i + 1])
                pend, now = [], pend
                for f in now:
                    f()
                final_e(b, h, t, "v" if i == 15 else "g")
                if ng < 16 and i > 3:
                    stage_gate(ng // 8, ng % 8)
                    ng += 1
                while nx < 8 and nsx <= i // 2:
                    xx = divmod(nx, 4)[0], divmod(nx, 4)[1] // 2, nx % 2
                    nx += 1
                    nsx += 1
                    stage_x(*xx, "ssss"[nx - 5])
                    pend.append(lambda xx=xx: quant_x(*xx))
                if t == 3:
                    store(b, h, 320 if b and h else 0)
                if t == 3 and i > 4:
                    store2(*items[i - 4][:2])
            store2(1, 1)
